import numpy as np, ml_dtypes
CORES = [7,39,87,119,135,167,215,247,263,295,343,375,391,423,471,503]
N = 16
NH, QP = 2, 128
def setup_inputs(rng):
    q = rng.standard_normal((N, 128, NH * QP), dtype=np.float32) / 4; k = rng.standard_normal((N, 128, NH * 128), dtype=np.float32)
    a = 2 * np.pi * rng.random((N, NH * QP)); s = 400 * rng.random((N, NH * QP)) ** 1.5; q[:, 0, :] = s * np.cos(a); q[:, 1, :] = s * np.sin(a); q[:, 2, :] = 150 * rng.standard_normal((N, NH * QP)); k[:, 2, :] = 1 + k[:, 2, :] / 50
    a = (2 * np.pi * rng.random((1, NH, 1)) + np.pi / 2 * (rng.permuted(np.tile(np.arange(N), (NH, 1)), axis=1).T.reshape(N, NH, 1) + 0.5) / N - 0.5 + rng.random((N, NH, 128))).reshape(N, NH * 128); k[:, 0, :] = np.cos(a); k[:, 1, :] = np.sin(a)
    return {"q": q.astype(ml_dtypes.bfloat16), "k": k.astype(ml_dtypes.bfloat16), "v": rng.standard_normal((N, 128, NH * 128), dtype=np.float32).astype(ml_dtypes.bfloat16)}
def setup_inputs_big(rng):
    d = setup_inputs(rng)
    for k in ("v",): d[k] = (d[k].astype(np.float32) * 1048576.0).astype(d[k].dtype)
    return d
def setup_inputs_small(rng):
    d = setup_inputs(rng)
    for k in ("v",): d[k] = (d[k].astype(np.float32) * (1 / 1048576.0)).astype(d[k].dtype)
    return d
def reference(q, k, v):
    Q, K, V = q.astype(np.float64), k.astype(np.float64), v.astype(np.float64)
    y = np.zeros((N, QP, NH * 128))
    for r in range(N):
        for h in range(NH):
            S = np.concatenate([K[j][:, 128 * h:128 * h + 128].T @ Q[r][:, QP * h:QP * h + QP] for j in range(N)], axis=0)
            P = np.exp(S - S.max(axis=0)); P = P / P.sum(axis=0)
            y[r][:, 128 * h:128 * h + 128] = P.T @ np.concatenate([V[j][:, 128 * h:128 * h + 128] for j in range(N)], axis=0)
    return {"y": y.astype(ml_dtypes.bfloat16)}

@@ -1,0 +1,351 @@
+from concourse.bass import DstId, RemoteDMATransfer
+from concourse.mybir import AluOpType, AxisListType, ActivationFunctionType
+
+NH = 2
+B = 128
+G = 4
+PKW = 136
+PKN = 130
+STAGES = [[0], [1, 2, 3]]
+NST = len(STAGES)
+
+SCRATCH = {
+    "own": ("sbuf", [128, 3 * B], "bfloat16"),
+    "st1": ("sbuf", [128, 3 * B], "bfloat16"),
+    "qf": ("sbuf", [128, G * B], "bfloat16"),
+    "kvf": ("sbuf", [128, G * 2 * B], "bfloat16"),
+    "ones": ("sbuf", [128, B], "bfloat16"),
+    "ident": ("sbuf", [128, B], "bfloat16"),
+    "P": ("sbuf", [128, G * G * B], "bfloat16"),
+    "PTs": ("sbuf", [128, G * G * B], "bfloat16"),
+    "Op": ("sbuf", [128, NST * G * B], "bfloat16"),
+    "Da": ("sbuf", [128, NST * G * B], "bfloat16"),
+    "pko": ("sbuf", [128, G * PKW], "bfloat16"),
+    "pk": ("sbuf", [128, NH * G * PKW], "bfloat16"),
+    "nmb": ("sbuf", [128, 64], "bfloat16"),
+    "sc": ("sbuf", [128, 64], "float32"),
+    "Dc": ("sbuf", [128, NH * G * B], "bfloat16"),
+    "ysb": ("sbuf", [128, NH * B], "bfloat16"),
+    "S0": ("psum", [128, 512], "float32"), "S1": ("psum", [128, 512], "float32"),
+    "S2": ("psum", [128, 512], "float32"), "S3": ("psum", [128, 512], "float32"),
+    "PT0": ("psum", [128, 1024], "bfloat16"), "PT1": ("psum", [128, 1024], "bfloat16"),
+    "PT2": ("psum", [128, 1024], "bfloat16"), "PT3": ("psum", [128, 1024], "bfloat16"),
+}
+_KINDS = ["sS", "sR", "sM", "sA", "sE", "sT", "sC", "sD", "sP", "sV", "sL"]
+SEMAPHORES = ([k + str(b) for k in _KINDS for b in range(G)] + ["qa%d" % i for i in range(G)]
+              + ["ka%d" % i for i in range(G)] + ["oarr", "ld0", "ld1", "lsem", "i1", "i2", "st"]
+              + [k + str(h) for k in ["pk", "cN", "cW", "cD", "cY", "cR", "cO"] for h in range(NH)])
+
+
+def _plan(T, topo):
+    cores = list(T.cores)
+    n = len(cores)
+    pos = [sorted(x for x in cores if topo.host(x) == topo.host(c)).index(c) for c in cores]
+
+    def rk(c):
+        return topo.rack(topo.host(c))
+
+    def near(a, b):
+        return topo.host(a) == topo.host(b) or (rk(a) != rk(b) and topo.may_write(a, b))
+
+    qg = [[s for s in range(n) if pos[s] % 2 == pos[r] % 2 and near(cores[r], cores[s])] for r in range(n)]
+    kg = [[s for s in range(n) if pos[s] // 2 == pos[r] // 2 and rk(cores[s]) == rk(cores[r])] for r in range(n)]
+
+    def helper(c):
+        for x in range(max(0, c - 16), c + 16):
+            if x != c and topo.host(x) == topo.host(c) and topo.chip(x) == topo.chip(c) and topo.die(x) != topo.die(c):
+                return x
+        return None
+
+    W = [cores, [helper(c) for c in cores]]
+    return cores, qg, kg, W
+
+
+def rank_program(g, core, T, topo):
+    cores, qg, kg, W = _plan(T, topo)
+    role = None
+    for hh in range(NH):
+        for rr in range(len(cores)):
+            if W[hh][rr] == core:
+                role = (hh, rr)
+    if role is None:
+        return
+    h, r = role
+    is_rank = h == 0
+    gq, gk = qg[r].index(r), kg[r].index(r)
+    te, ve, ac, sy = g.tensor, g.vector, g.scalar, g.sync
+    Exp, Copy = ActivationFunctionType.Exp, ActivationFunctionType.Copy
+    X = AxisListType.X
+    tot = {}
+
+    def inc(ins, name, n=1):
+        ins.then_inc(T.sem[name], n)
+        tot[name] = tot.get(name, 0) + n
+
+    def expect(name, n):
+        tot[name] = tot.get(name, 0) + n
+
+    def wait(q, name, v):
+        q.wait_ge(T.sem[name], v)
+
+    far = W[h][qg[r][(gq + 1) % G]]
+    mask = topo.mask(core, far)
+    ne = bin(mask).count("1")
+
+    def dst(c):
+        rid, pid = topo.addr(c, core)
+        return DstId(rid=rid, pnc=pid)
+
+    Sb = [T["S%d" % b] for b in range(G)]
+    PT = [T["PT%d" % b] for b in range(G)]
+    cumd = [sum(len(J) for J in STAGES[:s + 1]) for s in range(NST)]
+    cumP = [cumd[s] + s for s in range(NST)]
+    LAST = NST - 1
+    finL = max(NST - 1, 1)
+
+    def qAP(b):
+        return T.own[:, 0:B] if b == gq else T.qf[:, b * B:(b + 1) * B]
+
+    def kAP(d):
+        j = (gk - d) % G
+        return T.own[:, B:2 * B] if d == 0 else T.kvf[:, j * 2 * B:j * 2 * B + B]
+
+    def vAP(d):
+        j = (gk - d) % G
+        return T.own[:, 2 * B:3 * B] if d == 0 else T.kvf[:, j * 2 * B + B:(j + 1) * 2 * B]
+
+    def pkt(b):
+        return (T.pk, gq * PKW) if (is_rank and b == gq) else (T.pko, b * PKW)
+
+    def col(t, c):
+        return t[:, c:c + 1]
+
+    def nmAP(s, b):
+        if s == LAST:
+            t, o = pkt(b)
+            return col(t, o + B)
+        return col(T.nmb, s * G + b)
+
+    def bmAP(s, b):
+        return col(T.nmb, 32 + s * G + b)
+
+    def lacc(s, b):
+        return col(T.sc, s * G + b)
+
+    def ltot(s, b):
+        if s == LAST:
+            t, o = pkt(b)
+            return col(t, o + B + 1)
+        return lacc(0, b) if s == 0 else col(T.sc, 16 + s * G + b)
+
+    def alAP(s, b):
+        return col(T.sc, 32 + s * G + b)
+
+    def cols(t, b, s):
+        return t[:, b * G * B + STAGES[s][0] * B: b * G * B + (STAGES[s][-1] + 1) * B]
+
+    def blk(t, b, d):
+        return t[:, b * G * B + d * B: b * G * B + (d + 1) * B]
+
+    def sblk(t, s, b):
+        return t[:, (s * G + b) * B:(s * G + b + 1) * B]
+
+    def Scols(b, s):
+        return Sb[b][:, STAGES[s][0] * B:(STAGES[s][-1] + 1) * B]
+
+    def Oacc(b, s):
+        return Sb[b][:, STAGES[s][0] * B:(STAGES[s][0] + 1) * B]
+
+    arrive_order = [(gq - d) % G for d in range(G)]
+    send_order = [(gq + 1 + k) % G for k in range(G)]
+
+    def order(s):
+        return arrive_order if (s == 0 and NST > 1) else send_order
+
+    inc(ve.memset(T.ones[:], 1.0), "i1")
+    wait(g, "i1", 1)
+    inc(g.affine_select(T.ident[:], T.ones[:], [[-1, B]], AluOpType.is_equal, 0.0, 0, 1), "i2")
+
+    own_sem, own_val = ("ld0", 48) if is_rank else ("oarr", ne)
+    if is_rank:
+        inc(sy.dma_start(T.st1[:, 0:B], T.q[:, B:2 * B]), "ld1", 16)
+        inc(ac.dma_start(T.st1[:, B:2 * B], T.k[:, B:2 * B]), "ld1", 16)
+        inc(sy.dma_start(T.st1[:, 2 * B:3 * B], T.v[:, B:2 * B]), "ld1", 16)
+        inc(ac.dma_start(T.own[:, 0:B], T.q[:, 0:B]), "ld0", 16)
+        inc(sy.dma_start(T.own[:, B:2 * B], T.k[:, 0:B]), "ld0", 16)
+        inc(ac.dma_start(T.own[:, 2 * B:3 * B], T.v[:, 0:B]), "ld0", 16)
+        wait(g, "ld1", 48)
+        rid, pid = topo.addr(W[1][r], core)
+        g.remote_dma(out_ap=T.own[:], in_ap=T.st1[:], remote_sem=T.sem.oarr, local_sem=T.sem.lsem, pid=pid,
+                     routing_id=rid, dma_engine_mask=mask & topo.mask(core, W[1][r]))
+        expect("lsem", ne)
+    else:
+        expect("oarr", ne)
+
+    wait(g, own_sem, own_val)
+    qd = [W[h][qg[r][(gq + k) % G]] for k in range(1, G)]
+    kd = [W[h][kg[r][(gk + k) % G]] for k in range(1, G)]
+    g.remote_dma_fused([RemoteDMATransfer(dst_ids=[dst(c) for c in qd], dma_engine_mask=mask,
+                                          remote_sem=T.sem["qa%d" % gq], src=T.own[:, 0:B],
+                                          dsts=[T.qf[:, gq * B:(gq + 1) * B] for c in qd])], local_sem=T.sem.lsem)
+    g.remote_dma_fused([RemoteDMATransfer(dst_ids=[dst(c) for c in kd], dma_engine_mask=mask,
+                                          remote_sem=T.sem["ka%d" % gk], src=T.own[:, B:3 * B],
+                                          dsts=[T.kvf[:, gk * 2 * B:(gk + 1) * 2 * B] for c in kd])],
+                       local_sem=T.sem.lsem)
+    expect("lsem", 2 * ne)
+    for i in range(G):
+        if i != gq:
+            expect("qa%d" % i, ne)
+        if i != gk:
+            expect("ka%d" % i, ne)
+
+    seen = set()
+
+    def need(q, qn, name, v):
+        if (qn, name, v) not in seen:
+            seen.add((qn, name, v))
+            wait(q, name, v)
+
+    def need_q(b):
+        if b == gq:
+            need(te, "te", own_sem, own_val)
+        else:
+            need(te, "te", "qa%d" % b, ne)
+
+    def need_k(d):
+        if d == 0:
+            need(te, "te", own_sem, own_val)
+        else:
+            need(te, "te", "ka%d" % ((gk - d) % G), ne)
+
+    def S_mm(s, b, d):
+        inc(te.matmul(Sb[b][:, d * B:(d + 1) * B], qAP(b), kAP(d), True, True), "sS%d" % b)
+
+    def turn(s, b):
+        need(te, "te", "i2", 1)
+        wait(te, "sE%d" % b, s + 1)
+        for d in STAGES[s]:
+            inc(te.transpose(PT[b][:, d * B:(d + 1) * B], blk(T.P, b, d), T.ident[:]), "sT%d" % b)
+
+    def pv(s, b):
+        wait(te, "sC%d" % b, s + 1)
+        if s > 0:
+            wait(te, "sD%d" % b, s)
+            inc(te.matmul(Oacc(b, s), sblk(T.Da, s, b), sblk(T.Op, s - 1, b), True, False), "sP%d" % b)
+        for i, d in enumerate(STAGES[s]):
+            inc(te.matmul(Oacc(b, s), blk(T.PTs, b, d), vAP(d), s == 0 and i == 0, i == len(STAGES[s]) - 1),
+                "sP%d" % b)
+
+    def mx(s, b):
+        wait(ve, "sS%d" % b, cumd[s])
+        if s == 0:
+            inc(ve.tensor_reduce(nmAP(0, b), Scols(b, 0), X, AluOpType.max, negate=True), "sM%d" % b)
+        else:
+            inc(ve.tensor_reduce(bmAP(s, b), Scols(b, s), X, AluOpType.max, negate=True), "sR%d" % b)
+            wait(ve, "sR%d" % b, s)
+            wait(ve, "sM%d" % b, s)
+            inc(ve.tensor_tensor(nmAP(s, b), bmAP(s, b), nmAP(s - 1, b), AluOpType.min), "sM%d" % b)
+
+    def dg(s, b):
+        if s > 0:
+            need(ve, "ve", "i2", 1)
+            wait(ve, "sA%d" % b, s)
+            inc(ve.tensor_scalar(sblk(T.Da, s, b), T.ident[:], alAP(s, b), None, AluOpType.mult), "sD%d" % b)
+
+    def cp(s, b):
+        wait(ve, "sT%d" % b, cumd[s])
+        inc(ve.tensor_copy(cols(T.PTs, b, s), PT[b][:, STAGES[s][0] * B:(STAGES[s][-1] + 1) * B]), "sC%d" % b)
+        if s > 0:
+            wait(ve, "sE%d" % b, s + 1)
+            wait(ve, "sA%d" % b, s)
+            if s > 1:
+                wait(ve, "sL%d" % b, s - 1)
+            inc(ve.tensor_scalar(ltot(s, b), ltot(s - 1, b), alAP(s, b), lacc(s, b), AluOpType.mult, AluOpType.add),
+                "sL%d" % b)
+        elif NST == 1:
+            wait(ve, "sE%d" % b, 1)
+            inc(ve.tensor_copy(ltot(0, b), col(T.sc, 48 + b)), "sL%d" % b)
+
+    def ex(s, b):
+        wait(ac, "sM%d" % b, s + 1)
+        if s > 0:
+            inc(ac.activation(alAP(s, b), nmAP(s - 1, b), Exp, bias=nmAP(s, b), scale=-1.0), "sA%d" % b)
+        acc = col(T.sc, 48 + b) if NST == 1 else lacc(s, b)
+        inc(ac.activation(cols(T.P, b, s), Scols(b, s), Exp, bias=nmAP(s, b), scale=1.0, accum_out=acc), "sE%d" % b)
+
+    def ev(s, b):
+        wait(ac, "sP%d" % b, cumP[s])
+        if s == LAST:
+            t, o = pkt(b)
+            out = t[:, o:o + B]
+        else:
+            out = sblk(T.Op, s, b)
+        inc(ac.activation(out, Oacc(b, s), Copy), "sV%d" % b)
+
+    for s in range(NST):
+        o = order(s)
+        for i, d in enumerate(STAGES[s]):
+            need_k(d)
+            for b in o:
+                need_q(b)
+                if s > 0 and i == 0:
+                    wait(te, "sV%d" % b, s)
+                S_mm(s, b, d)
+        turn(s, o[0]); turn(s, o[1]); pv(s, o[0]); turn(s, o[2]); pv(s, o[1]); turn(s, o[3]); pv(s, o[2]); pv(s, o[3])
+        mx(s, o[0]); mx(s, o[1]); dg(s, o[0]); cp(s, o[0]); mx(s, o[2]); dg(s, o[1]); cp(s, o[1])
+        mx(s, o[3]); dg(s, o[2]); cp(s, o[2]); dg(s, o[3]); cp(s, o[3])
+        ex(s, o[0]); ex(s, o[1]); ex(s, o[2]); ev(s, o[0]); ex(s, o[3]); ev(s, o[1]); ev(s, o[2]); ev(s, o[3])
+
+    for b in send_order:
+        owner = cores[qg[r][b]]
+        if owner == core:
+            continue
+        wait(g, "sV%d" % b, NST)
+        wait(g, "sL%d" % b, finL)
+        wait(g, "sM%d" % b, NST)
+        rid, pid = topo.addr(owner, core)
+        slot = (h * G + gq) * PKW
+        g.remote_dma(out_ap=T.pk[:, slot:slot + PKN], in_ap=T.pko[:, b * PKW:b * PKW + PKN],
+                     remote_sem=T.sem["pk%d" % h], local_sem=T.sem.lsem, pid=pid, routing_id=rid,
+                     dma_engine_mask=mask & topo.mask(core, owner))
+        expect("lsem", ne)
+
+    if is_rank:
+        for hh in range(NH):
+            npk = ne * (G - 1 if hh == 0 else G)
+            expect("pk%d" % hh, npk)
+            base = hh * G * PKW
+            nms = T.pk[:, base + B: base + B + (G - 1) * PKW + 1: PKW]
+            nM, rL = col(T.sc, 52 + hh), col(T.sc, 54 + hh)
+            w = T.sc[:, 56 + hh * G: 56 + (hh + 1) * G]
+            yb = send_order[hh]
+            Y = Sb[yb][:, 2 * B:2 * B + PKN]
+            for q in (ve, ac, te):
+                wait(q, "pk%d" % hh, npk)
+                if hh == 0:
+                    wait(q, "sV%d" % gq, NST)
+                    wait(q, "sL%d" % gq, finL)
+                    wait(q, "sM%d" % gq, NST)
+            inc(ve.tensor_reduce(nM, nms, X, AluOpType.min), "cN%d" % hh)
+            wait(ac, "cN%d" % hh, 1)
+            inc(ac.activation(w, nms, Exp, bias=nM, scale=-1.0), "cW%d" % hh)
+            wait(ve, "cW%d" % hh, 1)
+            need(ve, "ve", "i2", 1)
+            for i in range(G):
+                inc(ve.tensor_scalar(T.Dc[:, (hh * G + i) * B:(hh * G + i + 1) * B], T.ident[:],
+                                     col(T.sc, 56 + hh * G + i), None, AluOpType.mult), "cD%d" % hh)
+            wait(te, "cD%d" % hh, G)
+            wait(te, "sV%d" % yb, NST)
+            for i in range(G):
+                inc(te.matmul(Y, T.Dc[:, (hh * G + i) * B:(hh * G + i + 1) * B],
+                              T.pk[:, base + i * PKW: base + i * PKW + PKN], i == 0, i == G - 1), "cY%d" % hh)
+            wait(ve, "cY%d" % hh, G)
+            inc(ve.reciprocal(rL, Sb[yb][:, 2 * B + B + 1:2 * B + B + 2]), "cR%d" % hh)
+            wait(ve, "cR%d" % hh, 1)
+            inc(ve.tensor_scalar(T.ysb[:, hh * B:(hh + 1) * B], Sb[yb][:, 2 * B:3 * B], rL, None, AluOpType.mult),
+                "cO%d" % hh)
+            wait(sy, "cO%d" % hh, 1)
+            inc(sy.dma_start(T.y[:, hh * B:(hh + 1) * B], T.ysb[:, hh * B:(hh + 1) * B]), "st", 16)
+
+    for name in sorted(tot):
+        wait(g, name, tot[name])

@@ -4,8 +4,7 @@ from concourse.mybir import AluOpType, AxisListType, ActivationFunctionType
 NH = 2
 B = 128
 G = 4
-PKW = 136
-PKN = 130
+MW = 8
 STAGES = [[0], [1, 2, 3]]
 NST = len(STAGES)
 
@@ -20,10 +19,12 @@ SCRATCH = {
     "PTs": ("sbuf", [128, G * G * B], "bfloat16"),
     "Op": ("sbuf", [128, NST * G * B], "bfloat16"),
     "Da": ("sbuf", [128, NST * G * B], "bfloat16"),
-    "pko": ("sbuf", [128, G * PKW], "bfloat16"),
-    "pk": ("sbuf", [128, NH * G * PKW], "bfloat16"),
+    "pko": ("sbuf", [128, G * B], "bfloat16"),
+    "pk": ("sbuf", [128, NH * G * B], "bfloat16"),
+    "mlo": ("sbuf", [128, G * MW], "bfloat16"),
+    "ml": ("sbuf", [128, NH * G * MW], "bfloat16"),
     "nmb": ("sbuf", [128, 64], "bfloat16"),
-    "sc": ("sbuf", [128, 64], "float32"),
+    "sc": ("sbuf", [128, 80], "float32"),
     "Dc": ("sbuf", [128, NH * G * B], "bfloat16"),
     "ysb": ("sbuf", [128, NH * B], "bfloat16"),
     "S0": ("psum", [128, 512], "float32"), "S1": ("psum", [128, 512], "float32"),
@@ -33,8 +34,9 @@ SCRATCH = {
 }
 _KINDS = ["sS", "sR", "sM", "sA", "sE", "sT", "sC", "sD", "sP", "sV", "sL"]
 SEMAPHORES = ([k + str(b) for k in _KINDS for b in range(G)] + ["qa%d" % i for i in range(G)]
-              + ["ka%d" % i for i in range(G)] + ["oarr", "ld0", "ld1", "lsem", "i1", "i2", "st"]
-              + [k + str(h) for k in ["pk", "cN", "cW", "cD", "cY", "cR", "cO"] for h in range(NH)])
+              + ["ka%d" % i for i in range(G)] + ["oarq", "oarr", "ld0", "ld1", "ldq", "lsem", "i1", "i2", "st"]
+              + [k + str(h) for k in ["ms", "cN", "cW", "cL", "cR", "cD", "cY", "cO"] for h in range(NH)]
+              + ["p%d%d" % (h, i) for h in range(NH) for i in range(G)])
 
 
 def _plan(T, topo):
@@ -88,8 +90,7 @@ def rank_program(g, core, T, topo):
     def wait(q, name, v):
         q.wait_ge(T.sem[name], v)
 
-    far = W[h][qg[r][(gq + 1) % G]]
-    mask = topo.mask(core, far)
+    mask = topo.mask(core, W[h][qg[r][(gq + 1) % G]])
     ne = bin(mask).count("1")
 
     def dst(c):
@@ -114,17 +115,20 @@ def rank_program(g, core, T, topo):
         j = (gk - d) % G
         return T.own[:, 2 * B:3 * B] if d == 0 else T.kvf[:, j * 2 * B + B:(j + 1) * 2 * B]
 
+    def home(b):
+        return is_rank and b == gq
+
     def pkt(b):
-        return (T.pk, gq * PKW) if (is_rank and b == gq) else (T.pko, b * PKW)
+        return T.pk[:, gq * B:(gq + 1) * B] if home(b) else T.pko[:, b * B:(b + 1) * B]
 
     def col(t, c):
         return t[:, c:c + 1]
 
+    def mlc(b, c):
+        return col(T.ml, gq * MW + c) if home(b) else col(T.mlo, b * MW + c)
+
     def nmAP(s, b):
-        if s == LAST:
-            t, o = pkt(b)
-            return col(t, o + B)
-        return col(T.nmb, s * G + b)
+        return mlc(b, 0) if s == LAST else col(T.nmb, s * G + b)
 
     def bmAP(s, b):
         return col(T.nmb, 32 + s * G + b)
@@ -134,8 +138,7 @@ def rank_program(g, core, T, topo):
 
     def ltot(s, b):
         if s == LAST:
-            t, o = pkt(b)
-            return col(t, o + B + 1)
+            return mlc(b, 1)
         return lacc(0, b) if s == 0 else col(T.sc, 16 + s * G + b)
 
     def alAP(s, b):
@@ -158,6 +161,7 @@ def rank_program(g, core, T, topo):
 
     arrive_order = [(gq - d) % G for d in range(G)]
     send_order = [(gq + 1 + k) % G for k in range(G)]
+    nb = G
 
     def order(s):
         return arrive_order if (s == 0 and NST > 1) else send_order
@@ -166,28 +170,35 @@ def rank_program(g, core, T, topo):
     wait(g, "i1", 1)
     inc(g.affine_select(T.ident[:], T.ones[:], [[-1, B]], AluOpType.is_equal, 0.0, 0, 1), "i2")
 
-    own_sem, own_val = ("ld0", 48) if is_rank else ("oarr", ne)
+    own_q = ("ld0", 48) if is_rank else ("oarq", ne)
+    own_kv = ("ld0", 48) if is_rank else ("oarr", ne)
     if is_rank:
-        inc(sy.dma_start(T.st1[:, 0:B], T.q[:, B:2 * B]), "ld1", 16)
+        inc(sy.dma_start(T.st1[:, 0:B], T.q[:, B:2 * B]), "ldq", 16)
         inc(ac.dma_start(T.st1[:, B:2 * B], T.k[:, B:2 * B]), "ld1", 16)
         inc(sy.dma_start(T.st1[:, 2 * B:3 * B], T.v[:, B:2 * B]), "ld1", 16)
         inc(ac.dma_start(T.own[:, 0:B], T.q[:, 0:B]), "ld0", 16)
         inc(sy.dma_start(T.own[:, B:2 * B], T.k[:, 0:B]), "ld0", 16)
         inc(ac.dma_start(T.own[:, 2 * B:3 * B], T.v[:, 0:B]), "ld0", 16)
-        wait(g, "ld1", 48)
         rid, pid = topo.addr(W[1][r], core)
-        g.remote_dma(out_ap=T.own[:], in_ap=T.st1[:], remote_sem=T.sem.oarr, local_sem=T.sem.lsem, pid=pid,
-                     routing_id=rid, dma_engine_mask=mask & topo.mask(core, W[1][r]))
-        expect("lsem", ne)
+        hm = mask & topo.mask(core, W[1][r])
+        wait(g, "ldq", 16)
+        g.remote_dma(out_ap=T.own[:, 0:B], in_ap=T.st1[:, 0:B], remote_sem=T.sem.oarq, local_sem=T.sem.lsem, pid=pid,
+                     routing_id=rid, dma_engine_mask=hm)
+        wait(g, "ld1", 32)
+        g.remote_dma(out_ap=T.own[:, B:3 * B], in_ap=T.st1[:, B:3 * B], remote_sem=T.sem.oarr, local_sem=T.sem.lsem,
+                     pid=pid, routing_id=rid, dma_engine_mask=hm)
+        expect("lsem", 2 * ne)
     else:
+        expect("oarq", ne)
         expect("oarr", ne)
 
-    wait(g, own_sem, own_val)
     qd = [W[h][qg[r][(gq + k) % G]] for k in range(1, G)]
     kd = [W[h][kg[r][(gk + k) % G]] for k in range(1, G)]
+    wait(g, own_q[0], own_q[1])
     g.remote_dma_fused([RemoteDMATransfer(dst_ids=[dst(c) for c in qd], dma_engine_mask=mask,
                                           remote_sem=T.sem["qa%d" % gq], src=T.own[:, 0:B],
                                           dsts=[T.qf[:, gq * B:(gq + 1) * B] for c in qd])], local_sem=T.sem.lsem)
+    wait(g, own_kv[0], own_kv[1])
     g.remote_dma_fused([RemoteDMATransfer(dst_ids=[dst(c) for c in kd], dma_engine_mask=mask,
                                           remote_sem=T.sem["ka%d" % gk], src=T.own[:, B:3 * B],
                                           dsts=[T.kvf[:, gk * 2 * B:(gk + 1) * 2 * B] for c in kd])],
@@ -208,13 +219,13 @@ def rank_program(g, core, T, topo):
 
     def need_q(b):
         if b == gq:
-            need(te, "te", own_sem, own_val)
+            need(te, "te", own_q[0], own_q[1])
         else:
             need(te, "te", "qa%d" % b, ne)
 
     def need_k(d):
         if d == 0:
-            need(te, "te", own_sem, own_val)
+            need(te, "te", own_kv[0], own_kv[1])
         else:
             need(te, "te", "ka%d" % ((gk - d) % G), ne)
 
@@ -275,12 +286,7 @@ def rank_program(g, core, T, topo):
 
     def ev(s, b):
         wait(ac, "sP%d" % b, cumP[s])
-        if s == LAST:
-            t, o = pkt(b)
-            out = t[:, o:o + B]
-        else:
-            out = sblk(T.Op, s, b)
-        inc(ac.activation(out, Oacc(b, s), Copy), "sV%d" % b)
+        inc(ac.activation(pkt(b) if s == LAST else sblk(T.Op, s, b), Oacc(b, s), Copy), "sV%d" % b)
 
     for s in range(NST):
         o = order(s)
@@ -291,59 +297,100 @@ def rank_program(g, core, T, topo):
                 if s > 0 and i == 0:
                     wait(te, "sV%d" % b, s)
                 S_mm(s, b, d)
-        turn(s, o[0]); turn(s, o[1]); pv(s, o[0]); turn(s, o[2]); pv(s, o[1]); turn(s, o[3]); pv(s, o[2]); pv(s, o[3])
-        mx(s, o[0]); mx(s, o[1]); dg(s, o[0]); cp(s, o[0]); mx(s, o[2]); dg(s, o[1]); cp(s, o[1])
-        mx(s, o[3]); dg(s, o[2]); cp(s, o[2]); dg(s, o[3]); cp(s, o[3])
-        ex(s, o[0]); ex(s, o[1]); ex(s, o[2]); ev(s, o[0]); ex(s, o[3]); ev(s, o[1]); ev(s, o[2]); ev(s, o[3])
+        turn(s, o[0])
+        for k in range(1, nb):
+            turn(s, o[k])
+            pv(s, o[k - 1])
+        pv(s, o[nb - 1])
+        mx(s, o[0])
+        mx(s, o[1])
+        for k in range(nb):
+            dg(s, o[k])
+            cp(s, o[k])
+            if k + 2 < nb:
+                mx(s, o[k + 2])
+        for k in range(min(3, nb)):
+            ex(s, o[k])
+        for k in range(nb):
+            ev(s, o[k])
+            if k + 3 < nb:
+                ex(s, o[k + 3])
 
-    for b in send_order:
+    def send_ml(b):
         owner = cores[qg[r][b]]
         if owner == core:
-            continue
-        wait(g, "sV%d" % b, NST)
+            return
         wait(g, "sL%d" % b, finL)
         wait(g, "sM%d" % b, NST)
         rid, pid = topo.addr(owner, core)
-        slot = (h * G + gq) * PKW
-        g.remote_dma(out_ap=T.pk[:, slot:slot + PKN], in_ap=T.pko[:, b * PKW:b * PKW + PKN],
-                     remote_sem=T.sem["pk%d" % h], local_sem=T.sem.lsem, pid=pid, routing_id=rid,
+        slot = (h * G + gq) * MW
+        g.remote_dma(out_ap=T.ml[:, slot:slot + 2], in_ap=T.mlo[:, b * MW:b * MW + 2], remote_sem=T.sem["ms%d" % h],
+                     local_sem=T.sem.lsem, pid=pid, routing_id=rid, dma_engine_mask=mask & topo.mask(core, owner))
+        expect("lsem", ne)
+
+    def send_pk(b):
+        owner = cores[qg[r][b]]
+        if owner == core:
+            return
+        wait(g, "sV%d" % b, NST)
+        rid, pid = topo.addr(owner, core)
+        slot = (h * G + gq) * B
+        g.remote_dma(out_ap=T.pk[:, slot:slot + B], in_ap=T.pko[:, b * B:(b + 1) * B],
+                     remote_sem=T.sem["p%d%d" % (h, gq)], local_sem=T.sem.lsem, pid=pid, routing_id=rid,
                      dma_engine_mask=mask & topo.mask(core, owner))
         expect("lsem", ne)
 
+    for k in range(min(3, nb)):
+        send_ml(send_order[k])
+    for k in range(nb):
+        send_pk(send_order[k])
+        if k + 3 < nb:
+            send_ml(send_order[k + 3])
+
     if is_rank:
         for hh in range(NH):
-            npk = ne * (G - 1 if hh == 0 else G)
-            expect("pk%d" % hh, npk)
-            base = hh * G * PKW
-            nms = T.pk[:, base + B: base + B + (G - 1) * PKW + 1: PKW]
-            nM, rL = col(T.sc, 52 + hh), col(T.sc, 54 + hh)
+            nms_ = ne * (G - 1 if hh == 0 else G)
+            expect("ms%d" % hh, nms_)
+            base = hh * G * MW
+            nms = T.ml[:, base: base + (G - 1) * MW + 1: MW]
+            ls = T.ml[:, base + 1: base + 1 + (G - 1) * MW + 1: MW]
+            nM, rL, L = col(T.sc, 52 + hh), col(T.sc, 54 + hh), col(T.sc, 72 + hh)
             w = T.sc[:, 56 + hh * G: 56 + (hh + 1) * G]
+            wl = T.sc[:, 64 + hh * G: 64 + (hh + 1) * G]
             yb = send_order[hh]
-            Y = Sb[yb][:, 2 * B:2 * B + PKN]
-            for q in (ve, ac, te):
-                wait(q, "pk%d" % hh, npk)
+            Y = Sb[yb][:, 2 * B:3 * B]
+            for q in (ve, ac):
+                wait(q, "ms%d" % hh, nms_)
                 if hh == 0:
-                    wait(q, "sV%d" % gq, NST)
                     wait(q, "sL%d" % gq, finL)
                     wait(q, "sM%d" % gq, NST)
             inc(ve.tensor_reduce(nM, nms, X, AluOpType.min), "cN%d" % hh)
             wait(ac, "cN%d" % hh, 1)
             inc(ac.activation(w, nms, Exp, bias=nM, scale=-1.0), "cW%d" % hh)
             wait(ve, "cW%d" % hh, 1)
+            inc(ve.tensor_tensor(wl, w, ls, AluOpType.mult), "cL%d" % hh)
+            wait(ve, "cL%d" % hh, 1)
+            inc(ve.tensor_reduce(L, wl, X, AluOpType.add), "cL%d" % hh)
+            wait(ve, "cL%d" % hh, 2)
+            inc(ve.reciprocal(rL, L), "cR%d" % hh)
+            wait(ve, "cR%d" % hh, 1)
             need(ve, "ve", "i2", 1)
             for i in range(G):
                 inc(ve.tensor_scalar(T.Dc[:, (hh * G + i) * B:(hh * G + i + 1) * B], T.ident[:],
-                                     col(T.sc, 56 + hh * G + i), None, AluOpType.mult), "cD%d" % hh)
+                                     col(T.sc, 56 + hh * G + i), rL, AluOpType.mult, AluOpType.mult), "cD%d" % hh)
             wait(te, "cD%d" % hh, G)
             wait(te, "sV%d" % yb, NST)
-            for i in range(G):
+            for k in range(G):
+                i = (gq - 1 - k) % G
+                if hh == 0 and i == gq:
+                    wait(te, "sV%d" % gq, NST)
+                else:
+                    expect("p%d%d" % (hh, i), ne)
+                    wait(te, "p%d%d" % (hh, i), ne)
                 inc(te.matmul(Y, T.Dc[:, (hh * G + i) * B:(hh * G + i + 1) * B],
-                              T.pk[:, base + i * PKW: base + i * PKW + PKN], i == 0, i == G - 1), "cY%d" % hh)
-            wait(ve, "cY%d" % hh, G)
-            inc(ve.reciprocal(rL, Sb[yb][:, 2 * B + B + 1:2 * B + B + 2]), "cR%d" % hh)
-            wait(ve, "cR%d" % hh, 1)
-            inc(ve.tensor_scalar(T.ysb[:, hh * B:(hh + 1) * B], Sb[yb][:, 2 * B:3 * B], rL, None, AluOpType.mult),
-                "cO%d" % hh)
+                              T.pk[:, (hh * G + i) * B:(hh * G + i + 1) * B], k == 0, k == G - 1), "cY%d" % hh)
+            wait(ac, "cY%d" % hh, G)
+            inc(ac.activation(T.ysb[:, hh * B:(hh + 1) * B], Y, Copy), "cO%d" % hh)
             wait(sy, "cO%d" % hh, 1)
             inc(sy.dma_start(T.y[:, hh * B:(hh + 1) * B], T.ysb[:, hh * B:(hh + 1) * B]), "st", 16)
 

@@ -5,8 +5,6 @@ NH = 2
 B = 128
 G = 4
 MW = 8
-STAGES = [[0], [1, 2, 3]]
-NST = len(STAGES)
 
 SCRATCH = {
     "own": ("sbuf", [128, 3 * B], "bfloat16"),
@@ -17,13 +15,10 @@ SCRATCH = {
     "ident": ("sbuf", [128, B], "bfloat16"),
     "P": ("sbuf", [128, G * G * B], "bfloat16"),
     "PTs": ("sbuf", [128, G * G * B], "bfloat16"),
-    "Op": ("sbuf", [128, NST * G * B], "bfloat16"),
-    "Da": ("sbuf", [128, NST * G * B], "bfloat16"),
     "pko": ("sbuf", [128, G * B], "bfloat16"),
     "pk": ("sbuf", [128, NH * G * B], "bfloat16"),
     "mlo": ("sbuf", [128, G * MW], "bfloat16"),
     "ml": ("sbuf", [128, NH * G * MW], "bfloat16"),
-    "nmb": ("sbuf", [128, 64], "bfloat16"),
     "sc": ("sbuf", [128, 80], "float32"),
     "Dc": ("sbuf", [128, NH * G * B], "bfloat16"),
     "ysb": ("sbuf", [128, NH * B], "bfloat16"),
@@ -32,9 +27,10 @@ SCRATCH = {
     "PT0": ("psum", [128, 1024], "bfloat16"), "PT1": ("psum", [128, 1024], "bfloat16"),
     "PT2": ("psum", [128, 1024], "bfloat16"), "PT3": ("psum", [128, 1024], "bfloat16"),
 }
-_KINDS = ["sS", "sR", "sM", "sA", "sE", "sT", "sC", "sD", "sP", "sV", "sL"]
+_KINDS = ["sS", "sM", "sE", "sT", "sC", "sP", "sV", "sL"]
 SEMAPHORES = ([k + str(b) for k in _KINDS for b in range(G)] + ["qa%d" % i for i in range(G)]
-              + ["ka%d" % i for i in range(G)] + ["oarq", "oarr", "ld0", "ld1", "ldq", "lsem", "i1", "i2", "st"]
+              + ["ka%d" % i for i in range(G)] + ["va%d" % i for i in range(G)]
+              + ["oarq", "oarr", "ld0", "ld1", "ldq", "lsem", "i1", "i2", "st"]
               + [k + str(h) for k in ["ms", "cN", "cW", "cL", "cR", "cD", "cY", "cO"] for h in range(NH)]
               + ["p%d%d" % (h, i) for h in range(NH) for i in range(G)])
 
@@ -99,10 +95,6 @@ def rank_program(g, core, T, topo):
 
     Sb = [T["S%d" % b] for b in range(G)]
     PT = [T["PT%d" % b] for b in range(G)]
-    cumd = [sum(len(J) for J in STAGES[:s + 1]) for s in range(NST)]
-    cumP = [cumd[s] + s for s in range(NST)]
-    LAST = NST - 1
-    finL = max(NST - 1, 1)
 
     def qAP(b):
         return T.own[:, 0:B] if b == gq else T.qf[:, b * B:(b + 1) * B]
@@ -127,44 +119,20 @@ def rank_program(g, core, T, topo):
     def mlc(b, c):
         return col(T.ml, gq * MW + c) if home(b) else col(T.mlo, b * MW + c)
 
-    def nmAP(s, b):
-        return mlc(b, 0) if s == LAST else col(T.nmb, s * G + b)
+    def lacc(b):
+        return col(T.sc, 48 + b)
 
-    def bmAP(s, b):
-        return col(T.nmb, 32 + s * G + b)
-
-    def lacc(s, b):
-        return col(T.sc, s * G + b)
-
-    def ltot(s, b):
-        if s == LAST:
-            return mlc(b, 1)
-        return lacc(0, b) if s == 0 else col(T.sc, 16 + s * G + b)
-
-    def alAP(s, b):
-        return col(T.sc, 32 + s * G + b)
-
-    def cols(t, b, s):
-        return t[:, b * G * B + STAGES[s][0] * B: b * G * B + (STAGES[s][-1] + 1) * B]
+    def row(t, b):
+        return t[:, b * G * B:(b + 1) * G * B]
 
     def blk(t, b, d):
         return t[:, b * G * B + d * B: b * G * B + (d + 1) * B]
 
-    def sblk(t, s, b):
-        return t[:, (s * G + b) * B:(s * G + b + 1) * B]
-
-    def Scols(b, s):
-        return Sb[b][:, STAGES[s][0] * B:(STAGES[s][-1] + 1) * B]
-
-    def Oacc(b, s):
-        return Sb[b][:, STAGES[s][0] * B:(STAGES[s][0] + 1) * B]
+    def Oacc(b):
+        return Sb[b][:, 0:B]
 
     arrive_order = [(gq - d) % G for d in range(G)]
-    send_order = [(gq + 1 + k) % G for k in range(G)]
-    nb = G
-
-    def order(s):
-        return arrive_order if (s == 0 and NST > 1) else send_order
+    o = [(gq + 1 + k) % G for k in range(G)]
 
     inc(ve.memset(T.ones[:], 1.0), "i1")
     wait(g, "i1", 1)
@@ -194,21 +162,24 @@ def rank_program(g, core, T, topo):
 
     qd = [W[h][qg[r][(gq + k) % G]] for k in range(1, G)]
     kd = [W[h][kg[r][(gk + k) % G]] for k in range(1, G)]
+
+    def spread(dsts_, sem, src, land):
+        g.remote_dma_fused([RemoteDMATransfer(dst_ids=[dst(c) for c in dsts_], dma_engine_mask=mask,
+                                              remote_sem=T.sem[sem], src=src, dsts=[land for c in dsts_])],
+                           local_sem=T.sem.lsem)
+        expect("lsem", ne)
+
     wait(g, own_q[0], own_q[1])
-    g.remote_dma_fused([RemoteDMATransfer(dst_ids=[dst(c) for c in qd], dma_engine_mask=mask,
-                                          remote_sem=T.sem["qa%d" % gq], src=T.own[:, 0:B],
-                                          dsts=[T.qf[:, gq * B:(gq + 1) * B] for c in qd])], local_sem=T.sem.lsem)
+    spread(qd, "qa%d" % gq, T.own[:, 0:B], T.qf[:, gq * B:(gq + 1) * B])
     wait(g, own_kv[0], own_kv[1])
-    g.remote_dma_fused([RemoteDMATransfer(dst_ids=[dst(c) for c in kd], dma_engine_mask=mask,
-                                          remote_sem=T.sem["ka%d" % gk], src=T.own[:, B:3 * B],
-                                          dsts=[T.kvf[:, gk * 2 * B:(gk + 1) * 2 * B] for c in kd])],
-                       local_sem=T.sem.lsem)
-    expect("lsem", 2 * ne)
+    spread(kd, "ka%d" % gk, T.own[:, B:2 * B], T.kvf[:, gk * 2 * B:gk * 2 * B + B])
+    spread(kd, "va%d" % gk, T.own[:, 2 * B:3 * B], T.kvf[:, gk * 2 * B + B:(gk + 1) * 2 * B])
     for i in range(G):
         if i != gq:
             expect("qa%d" % i, ne)
         if i != gk:
             expect("ka%d" % i, ne)
+            expect("va%d" % i, ne)
 
     seen = set()
 
@@ -223,129 +194,72 @@ def rank_program(g, core, T, topo):
         else:
             need(te, "te", "qa%d" % b, ne)
 
-    def need_k(d):
+    def need_kv(kind, d):
         if d == 0:
             need(te, "te", own_kv[0], own_kv[1])
         else:
-            need(te, "te", "ka%d" % ((gk - d) % G), ne)
+            need(te, "te", "%s%d" % (kind, (gk - d) % G), ne)
 
-    def S_mm(s, b, d):
-        inc(te.matmul(Sb[b][:, d * B:(d + 1) * B], qAP(b), kAP(d), True, True), "sS%d" % b)
-
-    def turn(s, b):
+    def turn(b):
         need(te, "te", "i2", 1)
-        wait(te, "sE%d" % b, s + 1)
-        for d in STAGES[s]:
+        wait(te, "sE%d" % b, 1)
+        for d in range(G):
             inc(te.transpose(PT[b][:, d * B:(d + 1) * B], blk(T.P, b, d), T.ident[:]), "sT%d" % b)
 
-    def pv(s, b):
-        wait(te, "sC%d" % b, s + 1)
-        if s > 0:
-            wait(te, "sD%d" % b, s)
-            inc(te.matmul(Oacc(b, s), sblk(T.Da, s, b), sblk(T.Op, s - 1, b), True, False), "sP%d" % b)
-        for i, d in enumerate(STAGES[s]):
-            inc(te.matmul(Oacc(b, s), blk(T.PTs, b, d), vAP(d), s == 0 and i == 0, i == len(STAGES[s]) - 1),
-                "sP%d" % b)
+    def pv(b, d):
+        need_kv("va", d)
+        need(te, "te", "sC%d" % b, 1)
+        inc(te.matmul(Oacc(b), blk(T.PTs, b, d), vAP(d), d == 0, d == G - 1), "sP%d" % b)
 
-    def mx(s, b):
-        wait(ve, "sS%d" % b, cumd[s])
-        if s == 0:
-            inc(ve.tensor_reduce(nmAP(0, b), Scols(b, 0), X, AluOpType.max, negate=True), "sM%d" % b)
-        else:
-            inc(ve.tensor_reduce(bmAP(s, b), Scols(b, s), X, AluOpType.max, negate=True), "sR%d" % b)
-            wait(ve, "sR%d" % b, s)
-            wait(ve, "sM%d" % b, s)
-            inc(ve.tensor_tensor(nmAP(s, b), bmAP(s, b), nmAP(s - 1, b), AluOpType.min), "sM%d" % b)
+    for d in range(G):
+        need_kv("ka", d)
+        for b in (arrive_order if d == 0 else o):
+            need_q(b)
+            inc(te.matmul(Sb[b][:, d * B:(d + 1) * B], qAP(b), kAP(d), True, True), "sS%d" % b)
+    turn(o[0])
+    for k in range(1, G):
+        turn(o[k])
+        pv(o[k - 1], 0)
+    pv(o[G - 1], 0)
+    for b in o:
+        pv(b, 1)
+    for b in o:
+        pv(b, 2)
+        pv(b, 3)
 
-    def dg(s, b):
-        if s > 0:
-            need(ve, "ve", "i2", 1)
-            wait(ve, "sA%d" % b, s)
-            inc(ve.tensor_scalar(sblk(T.Da, s, b), T.ident[:], alAP(s, b), None, AluOpType.mult), "sD%d" % b)
+    for b in o:
+        wait(ve, "sS%d" % b, G)
+        inc(ve.tensor_reduce(mlc(b, 0), Sb[b][:], X, AluOpType.max, negate=True), "sM%d" % b)
+    for b in o:
+        wait(ve, "sE%d" % b, 1)
+        inc(ve.tensor_copy(mlc(b, 1), lacc(b)), "sL%d" % b)
+        wait(ve, "sT%d" % b, G)
+        inc(ve.tensor_copy(row(T.PTs, b), PT[b][:, 0:G * B]), "sC%d" % b)
 
-    def cp(s, b):
-        wait(ve, "sT%d" % b, cumd[s])
-        inc(ve.tensor_copy(cols(T.PTs, b, s), PT[b][:, STAGES[s][0] * B:(STAGES[s][-1] + 1) * B]), "sC%d" % b)
-        if s > 0:
-            wait(ve, "sE%d" % b, s + 1)
-            wait(ve, "sA%d" % b, s)
-            if s > 1:
-                wait(ve, "sL%d" % b, s - 1)
-            inc(ve.tensor_scalar(ltot(s, b), ltot(s - 1, b), alAP(s, b), lacc(s, b), AluOpType.mult, AluOpType.add),
-                "sL%d" % b)
-        elif NST == 1:
-            wait(ve, "sE%d" % b, 1)
-            inc(ve.tensor_copy(ltot(0, b), col(T.sc, 48 + b)), "sL%d" % b)
+    for b in o:
+        wait(ac, "sM%d" % b, 1)
+        inc(ac.activation(row(T.P, b), Sb[b][:], Exp, bias=mlc(b, 0), scale=1.0, accum_out=lacc(b)), "sE%d" % b)
+    for b in o:
+        wait(ac, "sP%d" % b, G)
+        inc(ac.activation(pkt(b), Oacc(b), Copy), "sV%d" % b)
 
-    def ex(s, b):
-        wait(ac, "sM%d" % b, s + 1)
-        if s > 0:
-            inc(ac.activation(alAP(s, b), nmAP(s - 1, b), Exp, bias=nmAP(s, b), scale=-1.0), "sA%d" % b)
-        acc = col(T.sc, 48 + b) if NST == 1 else lacc(s, b)
-        inc(ac.activation(cols(T.P, b, s), Scols(b, s), Exp, bias=nmAP(s, b), scale=1.0, accum_out=acc), "sE%d" % b)
-
-    def ev(s, b):
-        wait(ac, "sP%d" % b, cumP[s])
-        inc(ac.activation(pkt(b) if s == LAST else sblk(T.Op, s, b), Oacc(b, s), Copy), "sV%d" % b)
-
-    for s in range(NST):
-        o = order(s)
-        for i, d in enumerate(STAGES[s]):
-            need_k(d)
-            for b in o:
-                need_q(b)
-                if s > 0 and i == 0:
-                    wait(te, "sV%d" % b, s)
-                S_mm(s, b, d)
-        turn(s, o[0])
-        for k in range(1, nb):
-            turn(s, o[k])
-            pv(s, o[k - 1])
-        pv(s, o[nb - 1])
-        mx(s, o[0])
-        mx(s, o[1])
-        for k in range(nb):
-            dg(s, o[k])
-            cp(s, o[k])
-            if k + 2 < nb:
-                mx(s, o[k + 2])
-        for k in range(min(3, nb)):
-            ex(s, o[k])
-        for k in range(nb):
-            ev(s, o[k])
-            if k + 3 < nb:
-                ex(s, o[k + 3])
-
-    def send_ml(b):
+    def send_home(b, sem_waits, out_ap, in_ap, sem):
         owner = cores[qg[r][b]]
         if owner == core:
             return
-        wait(g, "sL%d" % b, finL)
-        wait(g, "sM%d" % b, NST)
+        for name in sem_waits:
+            wait(g, name, 1)
         rid, pid = topo.addr(owner, core)
-        slot = (h * G + gq) * MW
-        g.remote_dma(out_ap=T.ml[:, slot:slot + 2], in_ap=T.mlo[:, b * MW:b * MW + 2], remote_sem=T.sem["ms%d" % h],
-                     local_sem=T.sem.lsem, pid=pid, routing_id=rid, dma_engine_mask=mask & topo.mask(core, owner))
-        expect("lsem", ne)
-
-    def send_pk(b):
-        owner = cores[qg[r][b]]
-        if owner == core:
-            return
-        wait(g, "sV%d" % b, NST)
-        rid, pid = topo.addr(owner, core)
-        slot = (h * G + gq) * B
-        g.remote_dma(out_ap=T.pk[:, slot:slot + B], in_ap=T.pko[:, b * B:(b + 1) * B],
-                     remote_sem=T.sem["p%d%d" % (h, gq)], local_sem=T.sem.lsem, pid=pid, routing_id=rid,
+        g.remote_dma(out_ap=out_ap, in_ap=in_ap, remote_sem=T.sem[sem], local_sem=T.sem.lsem, pid=pid, routing_id=rid,
                      dma_engine_mask=mask & topo.mask(core, owner))
         expect("lsem", ne)
 
-    for k in range(min(3, nb)):
-        send_ml(send_order[k])
-    for k in range(nb):
-        send_pk(send_order[k])
-        if k + 3 < nb:
-            send_ml(send_order[k + 3])
+    for b in o:
+        slot = (h * G + gq) * MW
+        send_home(b, ["sL%d" % b, "sM%d" % b], T.ml[:, slot:slot + 2], T.mlo[:, b * MW:b * MW + 2], "ms%d" % h)
+    for b in o:
+        slot = (h * G + gq) * B
+        send_home(b, ["sV%d" % b], T.pk[:, slot:slot + B], T.pko[:, b * B:(b + 1) * B], "p%d%d" % (h, gq))
 
     if is_rank:
         for hh in range(NH):
@@ -357,13 +271,11 @@ def rank_program(g, core, T, topo):
             nM, rL, L = col(T.sc, 52 + hh), col(T.sc, 54 + hh), col(T.sc, 72 + hh)
             w = T.sc[:, 56 + hh * G: 56 + (hh + 1) * G]
             wl = T.sc[:, 64 + hh * G: 64 + (hh + 1) * G]
-            yb = send_order[hh]
-            Y = Sb[yb][:, 2 * B:3 * B]
             for q in (ve, ac):
                 wait(q, "ms%d" % hh, nms_)
                 if hh == 0:
-                    wait(q, "sL%d" % gq, finL)
-                    wait(q, "sM%d" % gq, NST)
+                    wait(q, "sL%d" % gq, 1)
+                    wait(q, "sM%d" % gq, 1)
             inc(ve.tensor_reduce(nM, nms, X, AluOpType.min), "cN%d" % hh)
             wait(ac, "cN%d" % hh, 1)
             inc(ac.activation(w, nms, Exp, bias=nM, scale=-1.0), "cW%d" % hh)
@@ -378,12 +290,15 @@ def rank_program(g, core, T, topo):
             for i in range(G):
                 inc(ve.tensor_scalar(T.Dc[:, (hh * G + i) * B:(hh * G + i + 1) * B], T.ident[:],
                                      col(T.sc, 56 + hh * G + i), rL, AluOpType.mult, AluOpType.mult), "cD%d" % hh)
+        for hh in range(NH):
+            yb = o[hh]
+            Y = Sb[yb][:, 2 * B:3 * B]
             wait(te, "cD%d" % hh, G)
-            wait(te, "sV%d" % yb, NST)
+            wait(te, "sV%d" % yb, 1)
             for k in range(G):
                 i = (gq - 1 - k) % G
                 if hh == 0 and i == gq:
-                    wait(te, "sV%d" % gq, NST)
+                    wait(te, "sV%d" % gq, 1)
                 else:
                     expect("p%d%d" % (hh, i), ne)
                     wait(te, "p%d%d" % (hh, i), ne)

@@ -19,6 +19,7 @@ SCRATCH = {
     "pk": ("sbuf", [128, NH * G * B], "bfloat16"),
     "mlo": ("sbuf", [128, G * MW], "bfloat16"),
     "ml": ("sbuf", [128, NH * G * MW], "bfloat16"),
+    "ex": ("sbuf", [128, 2 * MW], "bfloat16"),
     "sc": ("sbuf", [128, 80], "float32"),
     "Dc": ("sbuf", [128, NH * G * B], "bfloat16"),
     "ysb": ("sbuf", [128, NH * B], "bfloat16"),
@@ -30,7 +31,8 @@ SCRATCH = {
 _KINDS = ["sS", "sM", "sE", "sT", "sC", "sP", "sV", "sL"]
 SEMAPHORES = ([k + str(b) for k in _KINDS for b in range(G)] + ["qa%d" % i for i in range(G)]
               + ["ka%d" % i for i in range(G)] + ["va%d" % i for i in range(G)]
-              + ["oarq", "oarr", "ld0", "ld1", "ldq", "lsem", "i1", "i2", "st"]
+              + ["oarq", "oark", "oarv", "ldq", "lq0", "lk0", "lv0", "lv1", "lsem", "i1", "i2", "st"]
+              + ["eS", "eM", "eE", "eX", "eF", "eP"]
               + [k + str(h) for k in ["ms", "cN", "cW", "cL", "cR", "cD", "cY", "cO"] for h in range(NH)]
               + ["p%d%d" % (h, i) for h in range(NH) for i in range(G)])
 
@@ -49,26 +51,39 @@ def _plan(T, topo):
     qg = [[s for s in range(n) if pos[s] % 2 == pos[r] % 2 and near(cores[r], cores[s])] for r in range(n)]
     kg = [[s for s in range(n) if pos[s] // 2 == pos[r] // 2 and rk(cores[s]) == rk(cores[r])] for r in range(n)]
 
-    def helper(c):
-        for x in range(max(0, c - 16), c + 16):
-            if x != c and topo.host(x) == topo.host(c) and topo.chip(x) == topo.chip(c) and topo.die(x) != topo.die(c):
-                return x
-        return None
+    def others(c):
+        return [x for x in range(max(0, c - 16), c + 16)
+                if x != c and topo.host(x) == topo.host(c) and topo.chip(x) == topo.chip(c) and topo.die(x) != topo.die(c)]
 
-    W = [cores, [helper(c) for c in cores]]
-    return cores, qg, kg, W
+    W = [cores, [others(c)[0] for c in cores]]
+    SQ = [others(c)[1] for c in cores]
+    SV = [others(c)[2] for c in cores]
+    return cores, qg, kg, W, SQ, SV
+
+
+def _halves(m):
+    bl = [1 << i for i in range(m.bit_length()) if (m >> i) & 1]
+    return sum(bl[:len(bl) // 2]), sum(bl[len(bl) // 2:])
+
+
+def _cnt(m):
+    return bin(m).count("1")
 
 
 def rank_program(g, core, T, topo):
-    cores, qg, kg, W = _plan(T, topo)
+    cores, qg, kg, W, SQ, SV = _plan(T, topo)
     role = None
-    for hh in range(NH):
-        for rr in range(len(cores)):
+    for rr in range(len(cores)):
+        for hh in range(NH):
             if W[hh][rr] == core:
-                role = (hh, rr)
+                role = (hh, rr, "w")
+        if SQ[rr] == core:
+            role = (1, rr, "q")
+        if SV[rr] == core:
+            role = (1, rr, "v")
     if role is None:
         return
-    h, r = role
+    h, r, job = role
     is_rank = h == 0
     gq, gk = qg[r].index(r), kg[r].index(r)
     te, ve, ac, sy = g.tensor, g.vector, g.scalar, g.sync
@@ -87,7 +102,10 @@ def rank_program(g, core, T, topo):
         q.wait_ge(T.sem[name], v)
 
     mask = topo.mask(core, W[h][qg[r][(gq + 1) % G]])
-    ne = bin(mask).count("1")
+    ne = _cnt(mask)
+    far = topo.mask(cores[r], cores[qg[r][(gq + 1) % G]])
+    inA, inB = _halves((topo.mask(cores[r], W[1][r]) & ~far) or far)
+    nA, nB = _cnt(inA), _cnt(inB)
 
     def dst(c):
         rid, pid = topo.addr(c, core)
@@ -131,49 +149,84 @@ def rank_program(g, core, T, topo):
     def Oacc(b):
         return Sb[b][:, 0:B]
 
+    nm0, nm1 = col(T.ex, 0), col(T.ex, MW)
+    fac, l0 = col(T.sc, 76), col(T.sc, 77)
+
     arrive_order = [(gq - d) % G for d in range(G)]
     o = [(gq + 1 + k) % G for k in range(G)]
+
+    qd = [W[h][qg[r][(gq + k) % G]] for k in range(1, G)]
+    kd = [W[h][kg[r][(gk + k) % G]] for k in range(1, G)]
+    oq, ok, ov = T.own[:, 0:B], T.own[:, B:2 * B], T.own[:, 2 * B:3 * B]
+
+    def xfer(dsts_, sem, src, land, m):
+        return (RemoteDMATransfer(dst_ids=[dst(c) for c in dsts_], dma_engine_mask=m, remote_sem=T.sem[sem], src=src,
+                                  dsts=[land for c in dsts_]), _cnt(m))
+
+    def call(xs):
+        g.remote_dma_fused([x for x, n in xs], local_sem=T.sem.lsem)
+        expect("lsem", sum(n for x, n in xs))
+
+    def xq(m):
+        return xfer(qd, "qa%d" % gq, oq, T.qf[:, gq * B:(gq + 1) * B], m)
+
+    def xk(m):
+        return xfer(kd, "ka%d" % gk, ok, T.kvf[:, gk * 2 * B:gk * 2 * B + B], m)
+
+    def xv(m):
+        return xfer(kd, "va%d" % gk, ov, T.kvf[:, gk * 2 * B + B:(gk + 1) * 2 * B], m)
+
+    def hand(dsts_, sem, j, m):
+        return xfer(dsts_, sem, T.st1[:, j * B:(j + 1) * B], T.own[:, j * B:(j + 1) * B], m)
+
+    def finish():
+        for name in sorted(tot):
+            wait(g, name, tot[name])
+
+    if job == "q":
+        expect("oarq", nA)
+        wait(g, "oarq", nA)
+        call([xq(mask)])
+        finish()
+        return
+    if job == "v":
+        expect("oarv", nB)
+        wait(g, "oarv", nB)
+        call([xv(mask)])
+        finish()
+        return
 
     inc(ve.memset(T.ones[:], 1.0), "i1")
     wait(g, "i1", 1)
     inc(g.affine_select(T.ident[:], T.ones[:], [[-1, B]], AluOpType.is_equal, 0.0, 0, 1), "i2")
 
-    own_q = ("ld0", 48) if is_rank else ("oarq", ne)
-    own_kv = ("ld0", 48) if is_rank else ("oarr", ne)
+    own_q = ("lq0", 16) if is_rank else ("oarq", nA)
+    own_k = ("lk0", 16) if is_rank else ("oark", nB)
+    own_v = ("lv0", 16) if is_rank else ("oarv", nA + nB)
     if is_rank:
         inc(sy.dma_start(T.st1[:, 0:B], T.q[:, B:2 * B]), "ldq", 16)
-        inc(ac.dma_start(T.st1[:, B:2 * B], T.k[:, B:2 * B]), "ld1", 16)
-        inc(sy.dma_start(T.st1[:, 2 * B:3 * B], T.v[:, B:2 * B]), "ld1", 16)
-        inc(ac.dma_start(T.own[:, 0:B], T.q[:, 0:B]), "ld0", 16)
-        inc(sy.dma_start(T.own[:, B:2 * B], T.k[:, 0:B]), "ld0", 16)
-        inc(ac.dma_start(T.own[:, 2 * B:3 * B], T.v[:, 0:B]), "ld0", 16)
-        rid, pid = topo.addr(W[1][r], core)
-        hm = mask & topo.mask(core, W[1][r])
-        wait(g, "ldq", 16)
-        g.remote_dma(out_ap=T.own[:, 0:B], in_ap=T.st1[:, 0:B], remote_sem=T.sem.oarq, local_sem=T.sem.lsem, pid=pid,
-                     routing_id=rid, dma_engine_mask=hm)
-        wait(g, "ld1", 32)
-        g.remote_dma(out_ap=T.own[:, B:3 * B], in_ap=T.st1[:, B:3 * B], remote_sem=T.sem.oarr, local_sem=T.sem.lsem,
-                     pid=pid, routing_id=rid, dma_engine_mask=hm)
-        expect("lsem", 2 * ne)
+        inc(ac.dma_start(T.st1[:, B:2 * B], T.k[:, B:2 * B]), "ldq", 16)
+        inc(sy.dma_start(oq, T.q[:, 0:B]), "lq0", 16)
+        inc(ac.dma_start(T.st1[:, 2 * B:3 * B], T.v[:, B:2 * B]), "lv1", 16)
+        inc(sy.dma_start(ok, T.k[:, 0:B]), "lk0", 16)
+        inc(ac.dma_start(ov, T.v[:, 0:B]), "lv0", 16)
+        wait(g, "ldq", 32)
+        call([hand([SQ[r]], "oarq", 0, inA), hand([W[1][r]], "oark", 1, inB)])
+        wait(g, "lq0", 16)
+        call([xq(mask)])
+        wait(g, "lv1", 16)
+        call([hand([W[1][r]], "oarq", 0, inA), hand([SV[r]], "oarv", 2, inB)])
+        wait(g, "lk0", 16)
+        call([xk(mask)])
+        wait(g, "lv0", 16)
+        call([xv(mask)])
+        call([hand([W[1][r]], "oarv", 2, inA + inB)])
     else:
-        expect("oarq", ne)
-        expect("oarr", ne)
-
-    qd = [W[h][qg[r][(gq + k) % G]] for k in range(1, G)]
-    kd = [W[h][kg[r][(gk + k) % G]] for k in range(1, G)]
-
-    def spread(dsts_, sem, src, land):
-        g.remote_dma_fused([RemoteDMATransfer(dst_ids=[dst(c) for c in dsts_], dma_engine_mask=mask,
-                                              remote_sem=T.sem[sem], src=src, dsts=[land for c in dsts_])],
-                           local_sem=T.sem.lsem)
-        expect("lsem", ne)
-
-    wait(g, own_q[0], own_q[1])
-    spread(qd, "qa%d" % gq, T.own[:, 0:B], T.qf[:, gq * B:(gq + 1) * B])
-    wait(g, own_kv[0], own_kv[1])
-    spread(kd, "ka%d" % gk, T.own[:, B:2 * B], T.kvf[:, gk * 2 * B:gk * 2 * B + B])
-    spread(kd, "va%d" % gk, T.own[:, 2 * B:3 * B], T.kvf[:, gk * 2 * B + B:(gk + 1) * 2 * B])
+        expect("oarq", nA)
+        expect("oark", nB)
+        expect("oarv", nA + nB)
+        wait(g, "oark", nB)
+        call([xk(mask)])
     for i in range(G):
         if i != gq:
             expect("qa%d" % i, ne)
@@ -194,15 +247,18 @@ def rank_program(g, core, T, topo):
         else:
             need(te, "te", "qa%d" % b, ne)
 
-    def need_kv(kind, d):
+    def need_kv(what, d):
         if d == 0:
-            need(te, "te", own_kv[0], own_kv[1])
+            ow = own_k if what == "ka" else own_v
+            need(te, "te", ow[0], ow[1])
         else:
-            need(te, "te", "%s%d" % (kind, (gk - d) % G), ne)
+            need(te, "te", "%s%d" % (what, (gk - d) % G), ne)
 
     def turn(b):
         need(te, "te", "i2", 1)
         wait(te, "sE%d" % b, 1)
+        if b == gq:
+            wait(te, "eP", 1)
         for d in range(G):
             inc(te.transpose(PT[b][:, d * B:(d + 1) * B], blk(T.P, b, d), T.ident[:]), "sT%d" % b)
 
@@ -215,30 +271,53 @@ def rank_program(g, core, T, topo):
         need_kv("ka", d)
         for b in (arrive_order if d == 0 else o):
             need_q(b)
-            inc(te.matmul(Sb[b][:, d * B:(d + 1) * B], qAP(b), kAP(d), True, True), "sS%d" % b)
+            if b == gq and d == 1:
+                wait(te, "eE", 1)
+            inc(te.matmul(Sb[b][:, d * B:(d + 1) * B], qAP(b), kAP(d), True, True),
+                "eS" if (b == gq and d == 0) else "sS%d" % b)
     turn(o[0])
     for k in range(1, G):
         turn(o[k])
-        pv(o[k - 1], 0)
-    pv(o[G - 1], 0)
-    for b in o:
-        pv(b, 1)
-    for b in o:
-        pv(b, 2)
-        pv(b, 3)
+        for d in range(G):
+            pv(o[k - 1], d)
+    for d in range(G):
+        pv(o[G - 1], d)
 
+    wait(ve, "eS", 1)
+    inc(ve.tensor_reduce(nm0, Sb[gq][:, 0:B], X, AluOpType.max, negate=True), "eM")
     for b in o:
-        wait(ve, "sS%d" % b, G)
-        inc(ve.tensor_reduce(mlc(b, 0), Sb[b][:], X, AluOpType.max, negate=True), "sM%d" % b)
+        if b == gq:
+            wait(ve, "sS%d" % b, G - 1)
+            inc(ve.tensor_reduce(nm1, Sb[b][:, B:G * B], X, AluOpType.max, negate=True), "eX")
+            wait(ve, "eX", 1)
+            wait(ve, "eM", 1)
+            inc(ve.tensor_tensor(mlc(b, 0), nm0, nm1, AluOpType.min), "sM%d" % b)
+        else:
+            wait(ve, "sS%d" % b, G)
+            inc(ve.tensor_reduce(mlc(b, 0), Sb[b][:], X, AluOpType.max, negate=True), "sM%d" % b)
     for b in o:
-        wait(ve, "sE%d" % b, 1)
-        inc(ve.tensor_copy(mlc(b, 1), lacc(b)), "sL%d" % b)
+        if b == gq:
+            wait(ve, "eF", 1)
+            wait(ve, "eE", 1)
+            inc(ve.tensor_scalar(blk(T.P, b, 0), blk(T.P, b, 0), fac, None, AluOpType.mult), "eP")
+            wait(ve, "sE%d" % b, 1)
+            inc(ve.tensor_scalar(mlc(b, 1), l0, fac, lacc(b), AluOpType.mult, AluOpType.add), "sL%d" % b)
+        else:
+            wait(ve, "sE%d" % b, 1)
+            inc(ve.tensor_copy(mlc(b, 1), lacc(b)), "sL%d" % b)
         wait(ve, "sT%d" % b, G)
         inc(ve.tensor_copy(row(T.PTs, b), PT[b][:, 0:G * B]), "sC%d" % b)
 
+    wait(ac, "eM", 1)
+    inc(ac.activation(blk(T.P, gq, 0), Sb[gq][:, 0:B], Exp, bias=nm0, scale=1.0, accum_out=l0), "eE")
     for b in o:
         wait(ac, "sM%d" % b, 1)
-        inc(ac.activation(row(T.P, b), Sb[b][:], Exp, bias=mlc(b, 0), scale=1.0, accum_out=lacc(b)), "sE%d" % b)
+        if b == gq:
+            inc(ac.activation(fac, nm0, Exp, bias=mlc(b, 0), scale=-1.0), "eF")
+            inc(ac.activation(T.P[:, b * G * B + B:(b + 1) * G * B], Sb[b][:, B:G * B], Exp, bias=mlc(b, 0), scale=1.0,
+                              accum_out=lacc(b)), "sE%d" % b)
+        else:
+            inc(ac.activation(row(T.P, b), Sb[b][:], Exp, bias=mlc(b, 0), scale=1.0, accum_out=lacc(b)), "sE%d" % b)
     for b in o:
         wait(ac, "sP%d" % b, G)
         inc(ac.activation(pkt(b), Oacc(b), Copy), "sV%d" % b)
@@ -309,5 +388,4 @@ def rank_program(g, core, T, topo):
             wait(sy, "cO%d" % hh, 1)
             inc(sy.dma_start(T.y[:, hh * B:(hh + 1) * B], T.ysb[:, hh * B:(hh + 1) * B]), "st", 16)
 
-    for name in sorted(tot):
-        wait(g, name, tot[name])
+    finish()

from concourse.bass import DstId, RemoteDMATransfer
from concourse.mybir import AluOpType, AxisListType, ActivationFunctionType

NH = 2
B = 128
G = 4
MW = 8

SCRATCH = {
    "own": ("sbuf", [128, 3 * B], "bfloat16"),
    "st1": ("sbuf", [128, 3 * B], "bfloat16"),
    "qf": ("sbuf", [128, G * B], "bfloat16"),
    "kvf": ("sbuf", [128, G * 2 * B], "bfloat16"),
    "ones": ("sbuf", [128, B], "bfloat16"),
    "ident": ("sbuf", [128, B], "bfloat16"),
    "P": ("sbuf", [128, G * G * B], "bfloat16"),
    "PTs": ("sbuf", [128, G * G * B], "bfloat16"),
    "pko": ("sbuf", [128, G * B], "bfloat16"),
    "pk": ("sbuf", [128, NH * G * B], "bfloat16"),
    "mlo": ("sbuf", [128, G * MW], "bfloat16"),
    "ml": ("sbuf", [128, NH * G * MW], "bfloat16"),
    "ex": ("sbuf", [128, 2 * MW], "bfloat16"),
    "sc": ("sbuf", [128, 80], "float32"),
    "Dc": ("sbuf", [128, NH * G * B], "bfloat16"),
    "ysb": ("sbuf", [128, NH * B], "bfloat16"),
    "S0": ("psum", [128, 512], "float32"), "S1": ("psum", [128, 512], "float32"),
    "S2": ("psum", [128, 512], "float32"), "S3": ("psum", [128, 512], "float32"),
    "PT0": ("psum", [128, 1024], "bfloat16"), "PT1": ("psum", [128, 1024], "bfloat16"),
    "PT2": ("psum", [128, 1024], "bfloat16"), "PT3": ("psum", [128, 1024], "bfloat16"),
}
_KINDS = ["sS", "sM", "sE", "sT", "sC", "sP", "sV", "sL"]
SEMAPHORES = ([k + str(b) for k in _KINDS for b in range(G)] + ["qa%d" % i for i in range(G)]
              + ["ka%d" % i for i in range(G)] + ["va%d" % i for i in range(G)]
              + ["oarq", "oark", "oarv", "ldq", "lq0", "lk0", "lv0", "lv1", "lsem", "i1", "i2", "st"]
              + ["eS", "eM", "eE", "eX", "eF", "eP"]
              + [k + str(h) for k in ["ms", "cN", "cW", "cL", "cR", "cD", "cY", "cO"] for h in range(NH)]
              + ["p%d%d" % (h, i) for h in range(NH) for i in range(G)])


def _plan(T, topo):
    cores = list(T.cores)
    n = len(cores)
    pos = [sorted(x for x in cores if topo.host(x) == topo.host(c)).index(c) for c in cores]

    def rk(c):
        return topo.rack(topo.host(c))

    def near(a, b):
        return topo.host(a) == topo.host(b) or (rk(a) != rk(b) and topo.may_write(a, b))

    qg = [[s for s in range(n) if pos[s] % 2 == pos[r] % 2 and near(cores[r], cores[s])] for r in range(n)]
    kg = [[s for s in range(n) if pos[s] // 2 == pos[r] // 2 and rk(cores[s]) == rk(cores[r])] for r in range(n)]

    def others(c):
        return [x for x in range(max(0, c - 16), c + 16)
                if x != c and topo.host(x) == topo.host(c) and topo.chip(x) == topo.chip(c) and topo.die(x) != topo.die(c)]

    W = [cores, [others(c)[0] for c in cores]]
    SQ = [others(c)[1] for c in cores]
    SV = [others(c)[2] for c in cores]
    return cores, qg, kg, W, SQ, SV


def _halves(m):
    bl = [1 << i for i in range(m.bit_length()) if (m >> i) & 1]
    return sum(bl[:len(bl) // 2]), sum(bl[len(bl) // 2:])


def _cnt(m):
    return bin(m).count("1")


def rank_program(g, core, T, topo):
    cores, qg, kg, W, SQ, SV = _plan(T, topo)
    role = None
    for rr in range(len(cores)):
        for hh in range(NH):
            if W[hh][rr] == core:
                role = (hh, rr, "w")
        if SQ[rr] == core:
            role = (1, rr, "q")
        if SV[rr] == core:
            role = (1, rr, "v")
    if role is None:
        return
    h, r, job = role
    is_rank = h == 0
    gq, gk = qg[r].index(r), kg[r].index(r)
    te, ve, ac, sy = g.tensor, g.vector, g.scalar, g.sync
    Exp, Copy = ActivationFunctionType.Exp, ActivationFunctionType.Copy
    X = AxisListType.X
    tot = {}

    def inc(ins, name, n=1):
        ins.then_inc(T.sem[name], n)
        tot[name] = tot.get(name, 0) + n

    def expect(name, n):
        tot[name] = tot.get(name, 0) + n

    def wait(q, name, v):
        q.wait_ge(T.sem[name], v)

    mask = topo.mask(core, W[h][qg[r][(gq + 1) % G]])
    ne = _cnt(mask)
    far = topo.mask(cores[r], cores[qg[r][(gq + 1) % G]])
    inA, inB = _halves((topo.mask(cores[r], W[1][r]) & ~far) or far)
    nA, nB = _cnt(inA), _cnt(inB)

    def dst(c):
        rid, pid = topo.addr(c, core)
        return DstId(rid=rid, pnc=pid)

    Sb = [T["S%d" % b] for b in range(G)]
    PT = [T["PT%d" % b] for b in range(G)]

    def qAP(b):
        return T.own[:, 0:B] if b == gq else T.qf[:, b * B:(b + 1) * B]

    def kAP(d):
        j = (gk - d) % G
        return T.own[:, B:2 * B] if d == 0 else T.kvf[:, j * 2 * B:j * 2 * B + B]

    def vAP(d):
        j = (gk - d) % G
        return T.own[:, 2 * B:3 * B] if d == 0 else T.kvf[:, j * 2 * B + B:(j + 1) * 2 * B]

    def home(b):
        return is_rank and b == gq

    def pkt(b):
        return T.pk[:, gq * B:(gq + 1) * B] if home(b) else T.pko[:, b * B:(b + 1) * B]

    def col(t, c):
        return t[:, c:c + 1]

    def mlc(b, c):
        return col(T.ml, gq * MW + c) if home(b) else col(T.mlo, b * MW + c)

    def lacc(b):
        return col(T.sc, 48 + b)

    def row(t, b):
        return t[:, b * G * B:(b + 1) * G * B]

    def blk(t, b, d):
        return t[:, b * G * B + d * B: b * G * B + (d + 1) * B]

    def Oacc(b):
        return Sb[b][:, 0:B]

    nm0, nm1 = col(T.ex, 0), col(T.ex, MW)
    fac, l0 = col(T.sc, 76), col(T.sc, 77)

    arrive_order = [(gq - d) % G for d in range(G)]
    o = [(gq + 1 + k) % G for k in range(G)]

    qd = [W[h][qg[r][(gq + k) % G]] for k in range(1, G)]
    kd = [W[h][kg[r][(gk + k) % G]] for k in range(1, G)]
    oq, ok, ov = T.own[:, 0:B], T.own[:, B:2 * B], T.own[:, 2 * B:3 * B]

    def xfer(dsts_, sem, src, land, m):
        return (RemoteDMATransfer(dst_ids=[dst(c) for c in dsts_], dma_engine_mask=m, remote_sem=T.sem[sem], src=src,
                                  dsts=[land for c in dsts_]), _cnt(m))

    def call(xs):
        g.remote_dma_fused([x for x, n in xs], local_sem=T.sem.lsem)
        expect("lsem", sum(n for x, n in xs))

    def xq(m):
        return xfer(qd, "qa%d" % gq, oq, T.qf[:, gq * B:(gq + 1) * B], m)

    def xk(m):
        return xfer(kd, "ka%d" % gk, ok, T.kvf[:, gk * 2 * B:gk * 2 * B + B], m)

    def xv(m):
        return xfer(kd, "va%d" % gk, ov, T.kvf[:, gk * 2 * B + B:(gk + 1) * 2 * B], m)

    def hand(dsts_, sem, j, m):
        return xfer(dsts_, sem, T.st1[:, j * B:(j + 1) * B], T.own[:, j * B:(j + 1) * B], m)

    def finish():
        for name in sorted(tot):
            wait(g, name, tot[name])

    if job == "q":
        expect("oarq", nA)
        wait(g, "oarq", nA)
        call([xq(mask)])
        finish()
        return
    if job == "v":
        expect("oarv", nB)
        wait(g, "oarv", nB)
        call([xv(mask)])
        finish()
        return

    inc(ve.memset(T.ones[:], 1.0), "i1")
    wait(g, "i1", 1)
    inc(g.affine_select(T.ident[:], T.ones[:], [[-1, B]], AluOpType.is_equal, 0.0, 0, 1), "i2")

    own_q = ("lq0", 16) if is_rank else ("oarq", nA)
    own_k = ("lk0", 16) if is_rank else ("oark", nB)
    own_v = ("lv0", 16) if is_rank else ("oarv", nA + nB)
    if is_rank:
        inc(sy.dma_start(T.st1[:, 0:B], T.q[:, B:2 * B]), "ldq", 16)
        inc(ac.dma_start(T.st1[:, B:2 * B], T.k[:, B:2 * B]), "ldq", 16)
        inc(sy.dma_start(oq, T.q[:, 0:B]), "lq0", 16)
        inc(ac.dma_start(T.st1[:, 2 * B:3 * B], T.v[:, B:2 * B]), "lv1", 16)
        inc(sy.dma_start(ok, T.k[:, 0:B]), "lk0", 16)
        inc(ac.dma_start(ov, T.v[:, 0:B]), "lv0", 16)
        wait(g, "ldq", 32)
        call([hand([SQ[r]], "oarq", 0, inA), hand([W[1][r]], "oark", 1, inB)])
        wait(g, "lq0", 16)
        call([xq(mask)])
        wait(g, "lv1", 16)
        call([hand([W[1][r]], "oarq", 0, inA), hand([SV[r]], "oarv", 2, inB)])
        wait(g, "lk0", 16)
        call([xk(mask)])
        wait(g, "lv0", 16)
        call([xv(mask)])
        call([hand([W[1][r]], "oarv", 2, inA + inB)])
    else:
        expect("oarq", nA)
        expect("oark", nB)
        expect("oarv", nA + nB)
        wait(g, "oark", nB)
        call([xk(mask)])
    for i in range(G):
        if i != gq:
            expect("qa%d" % i, ne)
        if i != gk:
            expect("ka%d" % i, ne)
            expect("va%d" % i, ne)

    seen = set()

    def need(q, qn, name, v):
        if (qn, name, v) not in seen:
            seen.add((qn, name, v))
            wait(q, name, v)

    def need_q(b):
        if b == gq:
            need(te, "te", own_q[0], own_q[1])
        else:
            need(te, "te", "qa%d" % b, ne)

    def need_kv(what, d):
        if d == 0:
            ow = own_k if what == "ka" else own_v
            need(te, "te", ow[0], ow[1])
        else:
            need(te, "te", "%s%d" % (what, (gk - d) % G), ne)

    def turn(b):
        need(te, "te", "i2", 1)
        wait(te, "sE%d" % b, 1)
        if b == gq:
            wait(te, "eP", 1)
        for d in range(G):
            inc(te.transpose(PT[b][:, d * B:(d + 1) * B], blk(T.P, b, d), T.ident[:]), "sT%d" % b)

    def pv(b, d):
        need_kv("va", d)
        need(te, "te", "sC%d" % b, 1)
        inc(te.matmul(Oacc(b), blk(T.PTs, b, d), vAP(d), d == 0, d == G - 1), "sP%d" % b)

    for d in range(G):
        need_kv("ka", d)
        for b in (arrive_order if d == 0 else o):
            need_q(b)
            if b == gq and d == 1:
                wait(te, "eE", 1)
            inc(te.matmul(Sb[b][:, d * B:(d + 1) * B], qAP(b), kAP(d), True, True),
                "eS" if (b == gq and d == 0) else "sS%d" % b)
    turn(o[0])
    for k in range(1, G):
        turn(o[k])
        for d in range(G):
            pv(o[k - 1], d)
    for d in range(G):
        pv(o[G - 1], d)

    wait(ve, "eS", 1)
    inc(ve.tensor_reduce(nm0, Sb[gq][:, 0:B], X, AluOpType.max, negate=True), "eM")
    for b in o:
        if b == gq:
            wait(ve, "sS%d" % b, G - 1)
            inc(ve.tensor_reduce(nm1, Sb[b][:, B:G * B], X, AluOpType.max, negate=True), "eX")
            wait(ve, "eX", 1)
            wait(ve, "eM", 1)
            inc(ve.tensor_tensor(mlc(b, 0), nm0, nm1, AluOpType.min), "sM%d" % b)
        else:
            wait(ve, "sS%d" % b, G)
            inc(ve.tensor_reduce(mlc(b, 0), Sb[b][:], X, AluOpType.max, negate=True), "sM%d" % b)
    for b in o:
        if b == gq:
            wait(ve, "eF", 1)
            wait(ve, "eE", 1)
            inc(ve.tensor_scalar(blk(T.P, b, 0), blk(T.P, b, 0), fac, None, AluOpType.mult), "eP")
            wait(ve, "sE%d" % b, 1)
            inc(ve.tensor_scalar(mlc(b, 1), l0, fac, lacc(b), AluOpType.mult, AluOpType.add), "sL%d" % b)
        else:
            wait(ve, "sE%d" % b, 1)
            inc(ve.tensor_copy(mlc(b, 1), lacc(b)), "sL%d" % b)
        wait(ve, "sT%d" % b, G)
        inc(ve.tensor_copy(row(T.PTs, b), PT[b][:, 0:G * B]), "sC%d" % b)

    wait(ac, "eM", 1)
    inc(ac.activation(blk(T.P, gq, 0), Sb[gq][:, 0:B], Exp, bias=nm0, scale=1.0, accum_out=l0), "eE")
    for b in o:
        wait(ac, "sM%d" % b, 1)
        if b == gq:
            inc(ac.activation(fac, nm0, Exp, bias=mlc(b, 0), scale=-1.0), "eF")
            inc(ac.activation(T.P[:, b * G * B + B:(b + 1) * G * B], Sb[b][:, B:G * B], Exp, bias=mlc(b, 0), scale=1.0,
                              accum_out=lacc(b)), "sE%d" % b)
        else:
            inc(ac.activation(row(T.P, b), Sb[b][:], Exp, bias=mlc(b, 0), scale=1.0, accum_out=lacc(b)), "sE%d" % b)
    for b in o:
        wait(ac, "sP%d" % b, G)
        inc(ac.activation(pkt(b), Oacc(b), Copy), "sV%d" % b)

    def send_home(b, sem_waits, out_ap, in_ap, sem):
        owner = cores[qg[r][b]]
        if owner == core:
            return
        for name in sem_waits:
            wait(g, name, 1)
        rid, pid = topo.addr(owner, core)
        g.remote_dma(out_ap=out_ap, in_ap=in_ap, remote_sem=T.sem[sem], local_sem=T.sem.lsem, pid=pid, routing_id=rid,
                     dma_engine_mask=mask & topo.mask(core, owner))
        expect("lsem", ne)

    for b in o:
        slot = (h * G + gq) * MW
        send_home(b, ["sL%d" % b, "sM%d" % b], T.ml[:, slot:slot + 2], T.mlo[:, b * MW:b * MW + 2], "ms%d" % h)
    for b in o:
        slot = (h * G + gq) * B
        send_home(b, ["sV%d" % b], T.pk[:, slot:slot + B], T.pko[:, b * B:(b + 1) * B], "p%d%d" % (h, gq))

    if is_rank:
        for hh in range(NH):
            nms_ = ne * (G - 1 if hh == 0 else G)
            expect("ms%d" % hh, nms_)
            base = hh * G * MW
            nms = T.ml[:, base: base + (G - 1) * MW + 1: MW]
            ls = T.ml[:, base + 1: base + 1 + (G - 1) * MW + 1: MW]
            nM, rL, L = col(T.sc, 52 + hh), col(T.sc, 54 + hh), col(T.sc, 72 + hh)
            w = T.sc[:, 56 + hh * G: 56 + (hh + 1) * G]
            wl = T.sc[:, 64 + hh * G: 64 + (hh + 1) * G]
            for q in (ve, ac):
                wait(q, "ms%d" % hh, nms_)
                if hh == 0:
                    wait(q, "sL%d" % gq, 1)
                    wait(q, "sM%d" % gq, 1)
            inc(ve.tensor_reduce(nM, nms, X, AluOpType.min), "cN%d" % hh)
            wait(ac, "cN%d" % hh, 1)
            inc(ac.activation(w, nms, Exp, bias=nM, scale=-1.0), "cW%d" % hh)
            wait(ve, "cW%d" % hh, 1)
            inc(ve.tensor_tensor(wl, w, ls, AluOpType.mult), "cL%d" % hh)
            wait(ve, "cL%d" % hh, 1)
            inc(ve.tensor_reduce(L, wl, X, AluOpType.add), "cL%d" % hh)
            wait(ve, "cL%d" % hh, 2)
            inc(ve.reciprocal(rL, L), "cR%d" % hh)
            wait(ve, "cR%d" % hh, 1)
            need(ve, "ve", "i2", 1)
            for i in range(G):
                inc(ve.tensor_scalar(T.Dc[:, (hh * G + i) * B:(hh * G + i + 1) * B], T.ident[:],
                                     col(T.sc, 56 + hh * G + i), rL, AluOpType.mult, AluOpType.mult), "cD%d" % hh)
        for hh in range(NH):
            yb = o[hh]
            Y = Sb[yb][:, 2 * B:3 * B]
            wait(te, "cD%d" % hh, G)
            wait(te, "sV%d" % yb, 1)
            for k in range(G):
                i = (gq - 1 - k) % G
                if hh == 0 and i == gq:
                    wait(te, "sV%d" % gq, 1)
                else:
                    expect("p%d%d" % (hh, i), ne)
                    wait(te, "p%d%d" % (hh, i), ne)
                inc(te.matmul(Y, T.Dc[:, (hh * G + i) * B:(hh * G + i + 1) * B],
                              T.pk[:, (hh * G + i) * B:(hh * G + i + 1) * B], k == 0, k == G - 1), "cY%d" % hh)
            wait(ac, "cY%d" % hh, G)
            inc(ac.activation(T.ysb[:, hh * B:(hh + 1) * B], Y, Copy), "cO%d" % hh)
            wait(sy, "cO%d" % hh, 1)
            inc(sy.dma_start(T.y[:, hh * B:(hh + 1) * B], T.ysb[:, hh * B:(hh + 1) * B]), "st", 16)

    finish()
